import numpy as np
import ml_dtypes


def mxq(x, axis, fmt="e4m3"):
    dtype, down = {"e4m3": (ml_dtypes.float8_e4m3fn, 7), "e5m2": (ml_dtypes.float8_e5m2, 14)}[fmt]
    v = np.moveaxis(np.asarray(x, np.float32).astype(ml_dtypes.bfloat16).astype(np.float64), axis, -1)
    blocks = v.reshape(v.shape[:-1] + (-1, 32))
    amax = np.abs(blocks).max(-1, keepdims=True)
    byte = np.maximum(np.where(amax > 0, np.frexp(amax)[1] - 1 + 127, 0) - down, 1)
    scale = np.exp2(byte - 127.0)
    codes = (blocks / scale).astype(np.float32).astype(dtype).astype(np.float64)
    return np.moveaxis((codes * scale).reshape(v.shape), -1, axis)


WIDE = False


def mx_kscale(k):
    if not WIDE:
        return np.ones(k)
    levels = np.array([10, -10, 5, -5, 0])
    if k % 512:
        return np.exp2(np.random.permutation(np.resize(levels, k // 32))).repeat(32)
    a = np.empty((k // 512, 16))
    for p in range(k // 512):
        a[p, :8] = np.random.permutation(np.resize(levels, 8))
        for g in range(8):
            far = levels[np.abs(levels - a[p, g]) >= 10]
            a[p, g + 8] = far[np.random.randint(len(far))]
    return np.exp2(a.ravel()).repeat(32)


def f64(x):
    return np.asarray(x).astype(np.float64)


def striped(idx):
    return np.tile(idx.reshape(-1, 16).T, (8, 1)).astype(np.uint16)


def unstriped(offs):
    return offs[:16].T.reshape(-1).astype(np.int64)


def pack_weight(w):
    k, n = w.shape
    w = f64(np.asarray(w, np.float32).astype(ml_dtypes.bfloat16)).reshape(k // 32, 32, n)
    amax = np.abs(w).max(1)
    byte = np.clip(np.where(amax > 0, np.frexp(amax)[1] - 1 + 127 - 7, 1), 1, 254)
    scaled = (w * np.exp2(127.0 - byte)[:, None, :]).reshape(k, n).astype(np.float32)
    words = np.ascontiguousarray(scaled.reshape(k // 512, 128, 4, n).transpose(0, 1, 3, 2)).astype(ml_dtypes.float8_e4m3fn).view(np.uint8)
    return words, np.ascontiguousarray(byte.astype(np.uint8).reshape(k // 512, 16, n))


def unpack_weight(words, scales):
    g, p, n, _ = words.shape
    vals = np.ascontiguousarray(words).view(ml_dtypes.float8_e4m3fn).astype(np.float64) * np.repeat(np.exp2(scales.astype(np.float64) - 127.0), 8, axis=1)[..., None]
    return vals.transpose(0, 1, 3, 2).reshape(g * 512, n)


K, T, S, N, H = 512, 2048, 512, 128, 512


def setup_inputs():
    n = np.random.standard_normal
    s = mx_kscale(K)[:, None]
    u = mx_kscale(H)
    packed_xT = pack_weight(n((K, T)) * s)
    return {
        "x_words": packed_xT[0],
        "x_scales": packed_xT[1],
        "hT": (n((K, H)) / np.sqrt(K) / s).astype(np.float32),
        "n2": (np.random.uniform(0.5, 1.5, (H, S))).astype(np.float32),
        "bw": (np.random.uniform(0.6, 1.4, (H, S))).astype(np.float32),
        "unit": (np.random.uniform(0.6, 1.4, (H, 1)) * u[:, None]).astype(np.float32),
        "w1": (n((H, N)) / np.sqrt(H) / u[:, None]).astype(np.float32),
        "offs": striped(np.random.permutation(T)[:S]),
        "sib": striped(np.random.permutation(S)),
    }


def reference(x_words, x_scales, hT, n2, bw, unit, w1, offs, sib):
    hTq = mxq(f64(hT), 0, "e4m3")
    xq = unpack_weight(x_words, x_scales)[:, unstriped(offs)]
    y = hTq.T @ xq
    dis = np.log(np.exp(f64(n2) - y) + 1.0)
    ker = f64(bw) / (dis + f64(bw))
    tot = ker.mean(axis=1, keepdims=True)
    wgt = ker / (tot + 0.2)
    ks = ker[:, unstriped(sib)]
    loo = ker - ks
    hid = f64(unit) * (wgt * loo)
    return mxq(f64(w1), 0, "e4m3").T @ mxq(hid, 0, "e4m3")

@@ -1,0 +1,151 @@
+from contextlib import ExitStack
+
+import concourse.mybir as mybir
+
+K, T, S, N, H = 512, 2048, 512, 128, 512
+FLOPS = 2 * K * H * S + 2 * H * N * S
+
+F32 = mybir.dt.float32
+BF16 = mybir.dt.bfloat16
+I32 = mybir.dt.int32
+U32 = mybir.dt.uint32
+U16 = mybir.dt.uint16
+U8 = mybir.dt.uint8
+FP8X4 = mybir.dt.float8_e4m3fn_x4
+ALU = mybir.AluOpType
+ACT = mybir.ActivationFunctionType
+
+P = 128
+PACK = 4
+TINY = 2.0 ** -60
+CHUNK = 128
+SCALAR_GATHERS = (3,)
+
+
+def tile_picked_ylandk_loo_p_kernel(tc, x_words, x_scales, hT, n2, bw, unit, w1, offs, sib, out):
+    nc = tc.nc
+    with ExitStack() as ctx:
+        keep = ctx.enter_context(tc.tile_pool(name="keep", bufs=1))
+        psum = ctx.enter_context(tc.psum_pool(name="psum", bufs=1))
+
+        offs_t = keep.tile([P, S // 16], U16, name="offs_t")
+        sib_t = keep.tile([P, S // 16], U16, name="sib_t")
+        xw = keep.tile([P, T], U32, name="xw", align_bytes=64)
+        xs = keep.tile([P, T], U8, name="xs", align_bytes=64)
+        h_raw = keep.tile([P, PACK, H], F32, name="h_raw", align_bytes=64)
+        w_raw = keep.tile([P, PACK, N], F32, name="w_raw", align_bytes=64)
+        unit_t = keep.tile([P, PACK], F32, name="unit_t")
+        n2_t = [keep.tile([P, S], F32, name=f"n2_{t}", align_bytes=64) for t in range(PACK)]
+        bw_t = [keep.tile([P, S], F32, name=f"bw_{t}", align_bytes=64) for t in range(PACK)]
+
+        nc.vector.memset(xs[:].bitcast(I32), 0)
+        nc.sync.dma_start(offs_t[:], offs)
+        nc.sync.dma_start(h_raw[:], hT.rearrange("(p j) c -> p j c", j=PACK))
+        for q in range(4):
+            nc.scalar.dma_start(xs[32 * q : 32 * q + 4, :].bitcast(I32), x_scales[0, 4 * q : 4 * q + 4, :].bitcast(I32))
+        nc.sync.dma_start(xw[:].bitcast(I32), x_words[0].rearrange("p n r -> p (n r)").bitcast(I32))
+        n2_v = n2.rearrange("(p t) j -> p t j", t=PACK)
+        bw_v = bw.rearrange("(p t) j -> p t j", t=PACK)
+        for t in range(PACK):
+            nc.sync.dma_start(n2_t[t][:], n2_v[:, t, :])
+        nc.sync.dma_start(w_raw[:], w1.rearrange("(p t) n -> p t n", t=PACK))
+        for t in range(PACK):
+            nc.sync.dma_start(bw_t[t][:], bw_v[:, t, :])
+        nc.sync.dma_start(sib_t[:], sib)
+        nc.sync.dma_start(unit_t[:], unit.rearrange("(p t) o -> p (t o)", t=PACK))
+
+        gs = keep.tile([P, S], U8, name="gs", align_bytes=64)
+        gw = keep.tile([P, S], U32, name="gw", align_bytes=64)
+        nc.vector.tensor_copy(gs[:], xs[:].indirect(offs_t[:]))
+
+        hq = keep.tile([P, PACK, P, PACK], BF16, name="hq", align_bytes=64)
+        src = h_raw[:].rearrange("p j (m t) -> p m j t", t=PACK)
+        dst = hq[:].rearrange("p t m j -> p m j t")
+        cut = 80
+        nc.scalar.copy(dst[:, cut:, :, :], src[:, cut:, :, :])
+        nc.vector.tensor_copy(dst[:, :cut, :, :], src[:, :cut, :, :])
+        hc = keep.tile([P, H], U32, name="hc", align_bytes=64)
+        hs = keep.tile([P, H], U8, name="hs", align_bytes=64)
+        nc.vector.quantize_mx(out=hc[:].bitcast(FP8X4), scales=hs[:], in_=hq[:].rearrange("p t m j -> p (t m j)"))
+        nc.vector.tensor_copy(gw[:], xw[:].indirect(offs_t[:]))
+
+        y = [psum.tile([P, S], F32, name=f"y{t}") for t in range(PACK)]
+        nd = keep.tile([P, PACK, S], F32, name="nd", align_bytes=64)
+        sg = keep.tile([P, PACK, S], F32, name="sg", align_bytes=64)
+        for t in range(PACK):
+            cols = slice(t * P, (t + 1) * P)
+            nc.tensor.matmul_mx(out=y[t][:], lhsT=hc[:, cols].bitcast(FP8X4), lhsT_scale=hs[:, cols],
+                                rhs=gw[:].bitcast(FP8X4), rhs_scale=gs[:], start=True, stop=True)
+        for t in range(PACK):
+            nc.vector.tensor_tensor(nd[:, t, :], y[t][:], n2_t[t][:], ALU.subtract)
+            nc.scalar.activation(sg[:, t, :], nd[:, t, :], ACT.Sigmoid)
+
+        wq = keep.tile([P, N, PACK], BF16, name="wq", align_bytes=64)
+        wc = keep.tile([P, N], U32, name="wc", align_bytes=64)
+        ws = keep.tile([P, N], U8, name="ws", align_bytes=64)
+        nc.vector.tensor_copy(wq[:].rearrange("p (c i) t -> p c t i", i=4), w_raw[:].rearrange("p t (c i) -> p c t i", i=4))
+        nc.vector.quantize_mx(out=wc[:].bitcast(FP8X4), scales=ws[:], in_=wq[:].rearrange("p n t -> p (n t)"))
+
+        lg = keep.tile([P, PACK, S], F32, name="lg", align_bytes=64)
+        ndis = keep.tile([P, PACK, S], F32, name="ndis", align_bytes=64)
+        zz = [keep.tile([P, 2 * S], F32, name=f"zz{t}", align_bytes=64) for t in range(PACK)]
+        zs = [keep.tile([P, S], F32, name=f"zs{t}", align_bytes=64) for t in range(PACK)]
+        for c in range(S // CHUNK):
+            cols = slice(c * CHUNK, (c + 1) * CHUNK)
+            nc.scalar.activation(lg[:, :, cols], sg[:, :, cols], ACT.Ln, bias=TINY)
+            nc.vector.scalar_tensor_tensor(ndis[:, :, cols], lg[:, :, cols], -TINY, nd[:, :, cols], ALU.min, ALU.min)
+        for t in range(PACK):
+            nc.scalar.activation(sg[:, t, :], bw_t[t][:], ACT.Ln)
+            nc.scalar.activation(zz[t][:, S:], ndis[:, t, :], ACT.Ln, scale=-1.0)
+            nc.vector.tensor_tensor(zz[t][:, :S], sg[:, t, :], zz[t][:, S:], ALU.subtract)
+            if t not in SCALAR_GATHERS:
+                nc.vector.tensor_copy(zs[t][:], zz[t][:].indirect(sib_t[:]))
+
+        ker = [keep.tile([P, S], F32, name=f"ker{t}", align_bytes=64) for t in range(PACK)]
+        ks = [keep.tile([P, S], F32, name=f"ks{t}", align_bytes=64) for t in range(PACK)]
+        loo = [keep.tile([P, S], F32, name=f"loo{t}", align_bytes=64) for t in range(PACK)]
+        hid = keep.tile([P, PACK, S], BF16, name="hid", align_bytes=64)
+        for pair in range(2):
+            tot = keep.tile([P, 2], F32, name=f"tot{pair}")
+            den = keep.tile([P, 2], F32, name=f"den{pair}")
+            inv = keep.tile([P, 2], F32, name=f"inv{pair}")
+            fac = keep.tile([P, 2], F32, name=f"fac{pair}")
+            t0, t1 = 2 * pair, 2 * pair + 1
+            for u, t in enumerate((t0, t1)):
+                nc.scalar.activation(ker[t][:], zz[t][:, :S], ACT.Sigmoid, accum_out=tot[:, u : u + 1])
+                if t in SCALAR_GATHERS:
+                    nc.scalar.activation(ks[t][:], zz[t][:].indirect(sib_t[:]), ACT.Sigmoid)
+                else:
+                    nc.scalar.activation(ks[t][:], zs[t][:], ACT.Sigmoid)
+            nc.vector.tensor_tensor(loo[t0][:], ker[t0][:], ks[t0][:], ALU.subtract)
+            nc.vector.tensor_scalar(den[:], tot[:], 0.2 * S, None, ALU.add)
+            nc.vector.reciprocal(inv[:], den[:])
+            nc.vector.scalar_tensor_tensor(fac[:], inv[:], float(S), unit_t[:, t0 : t1 + 1], ALU.mult, ALU.mult)
+            nc.vector.tensor_tensor(loo[t1][:], ker[t1][:], ks[t1][:], ALU.subtract)
+            nc.vector.scalar_tensor_tensor(hid[:, t0, :], loo[t0][:], fac[:, 0:1], ker[t0][:], ALU.mult, ALU.mult)
+            halves = (slice(0, S),) if pair == 0 else (slice(0, S // 2), slice(S // 2, S))
+            for cols in halves:
+                nc.vector.scalar_tensor_tensor(hid[:, t1, cols], loo[t1][:, cols], fac[:, 1:2], ker[t1][:, cols], ALU.mult, ALU.mult)
+
+        res = keep.tile([P, S], F32, name="res", align_bytes=64)
+        woven = [keep.tile([P, CHUNK, PACK], BF16, name=f"woven{c}", align_bytes=64) for c in range(S // CHUNK)]
+        for c in range(S // CHUNK):
+            cols = slice(c * CHUNK, (c + 1) * CHUNK)
+            wdst = woven[c][:].rearrange("p (c i) t -> p c t i", i=4)
+            wsrc = hid[:, :, cols].rearrange("p t (c i) -> p c t i", i=4)
+            if c % 2 == 0:
+                nc.scalar.copy(wdst, wsrc)
+            else:
+                nc.vector.tensor_copy(wdst, wsrc)
+        for c in range(S // CHUNK):
+            cols = slice(c * CHUNK, (c + 1) * CHUNK)
+            qc = keep.tile([P, CHUNK], U32, name=f"qc{c}", align_bytes=64)
+            qs = keep.tile([P, CHUNK], U8, name=f"qs{c}", align_bytes=64)
+            acc = psum.tile([P, CHUNK], F32, name=f"acc{c}")
+            nc.vector.quantize_mx(out=qc[:].bitcast(FP8X4), scales=qs[:], in_=woven[c][:].rearrange("p n t -> p (n t)"))
+            nc.tensor.matmul_mx(out=acc[:], lhsT=wc[:].bitcast(FP8X4), lhsT_scale=ws[:],
+                                rhs=qc[:].bitcast(FP8X4), rhs_scale=qs[:], start=True, stop=True)
+            nc.scalar.copy(res[:, cols], acc[:])
+            if c % 2 == 1:
+                both = slice((c - 1) * CHUNK, (c + 1) * CHUNK)
+                nc.sync.dma_start(out[:, both], res[:, both])

@@ -19,6 +19,7 @@ P = 128
 PACK = 4
 TINY = 2.0 ** -60
 CHUNK = 128
+HALF = S // 2
 SCALAR_GATHERS = (3,)
 
 
@@ -35,27 +36,27 @@ def tile_picked_ylandk_loo_p_kernel(tc, x_words, x_scales, hT, n2, bw, unit, w1,
         h_raw = keep.tile([P, PACK, H], F32, name="h_raw", align_bytes=64)
         w_raw = keep.tile([P, PACK, N], F32, name="w_raw", align_bytes=64)
         unit_t = keep.tile([P, PACK], F32, name="unit_t")
-        n2_t = [keep.tile([P, S], F32, name=f"n2_{t}", align_bytes=64) for t in range(PACK)]
+        n2_t = [keep.tile([P, 2, S], F32, name=f"n2_{u}", align_bytes=64) for u in range(2)]
         bw_t = [keep.tile([P, S], F32, name=f"bw_{t}", align_bytes=64) for t in range(PACK)]
 
         nc.vector.memset(xs[:].bitcast(I32), 0)
         nc.sync.dma_start(offs_t[:], offs)
         nc.sync.dma_start(h_raw[:], hT.rearrange("(p j) c -> p j c", j=PACK))
         for q in range(4):
-            nc.scalar.dma_start(xs[32 * q : 32 * q + 4, :].bitcast(I32), x_scales[0, 4 * q : 4 * q + 4, :].bitcast(I32))
+            nc.sync.dma_start(xs[32 * q : 32 * q + 4, :].bitcast(I32), x_scales[0, 4 * q : 4 * q + 4, :].bitcast(I32))
         nc.sync.dma_start(xw[:].bitcast(I32), x_words[0].rearrange("p n r -> p (n r)").bitcast(I32))
         n2_v = n2.rearrange("(p t) j -> p t j", t=PACK)
         bw_v = bw.rearrange("(p t) j -> p t j", t=PACK)
-        for t in range(PACK):
-            nc.sync.dma_start(n2_t[t][:], n2_v[:, t, :])
+        for u in range(2):
+            nc.sync.dma_start(n2_t[u][:], n2_v[:, 2 * u : 2 * u + 2, :])
         nc.sync.dma_start(w_raw[:], w1.rearrange("(p t) n -> p t n", t=PACK))
+        nc.sync.dma_start(unit_t[:], unit.rearrange("(p t) o -> p (t o)", t=PACK))
         for t in range(PACK):
             nc.sync.dma_start(bw_t[t][:], bw_v[:, t, :])
         nc.sync.dma_start(sib_t[:], sib)
-        nc.sync.dma_start(unit_t[:], unit.rearrange("(p t) o -> p (t o)", t=PACK))
 
         gs = keep.tile([P, S], U8, name="gs", align_bytes=64)
-        gw = keep.tile([P, S], U32, name="gw", align_bytes=64)
+        gw = [keep.tile([P, HALF], U32, name=f"gw{h}", align_bytes=64) for h in range(2)]
         nc.vector.tensor_copy(gs[:], xs[:].indirect(offs_t[:]))
 
         hq = keep.tile([P, PACK, P, PACK], BF16, name="hq", align_bytes=64)
@@ -67,18 +68,22 @@ def tile_picked_ylandk_loo_p_kernel(tc, x_words, x_scales, hT, n2, bw, unit, w1,
         hc = keep.tile([P, H], U32, name="hc", align_bytes=64)
         hs = keep.tile([P, H], U8, name="hs", align_bytes=64)
         nc.vector.quantize_mx(out=hc[:].bitcast(FP8X4), scales=hs[:], in_=hq[:].rearrange("p t m j -> p (t m j)"))
-        nc.vector.tensor_copy(gw[:], xw[:].indirect(offs_t[:]))
+        for h in range(2):
+            nc.vector.tensor_copy(gw[h][:], xw[:].indirect(offs_t[:, h * HALF // 16 : (h + 1) * HALF // 16]))
 
-        y = [psum.tile([P, S], F32, name=f"y{t}") for t in range(PACK)]
         nd = keep.tile([P, PACK, S], F32, name="nd", align_bytes=64)
         sg = keep.tile([P, PACK, S], F32, name="sg", align_bytes=64)
-        for t in range(PACK):
-            cols = slice(t * P, (t + 1) * P)
-            nc.tensor.matmul_mx(out=y[t][:], lhsT=hc[:, cols].bitcast(FP8X4), lhsT_scale=hs[:, cols],
-                                rhs=gw[:].bitcast(FP8X4), rhs_scale=gs[:], start=True, stop=True)
-        for t in range(PACK):
-            nc.vector.tensor_tensor(nd[:, t, :], y[t][:], n2_t[t][:], ALU.subtract)
-            nc.scalar.activation(sg[:, t, :], nd[:, t, :], ACT.Sigmoid)
+        for u in range(2):
+            pair = slice(2 * u, 2 * u + 2)
+            for h in range(2):
+                half = slice(h * HALF, (h + 1) * HALF)
+                y = psum.tile([P, 2, HALF], F32, name=f"y{u}{h}")
+                for e in range(2):
+                    cols = slice((2 * u + e) * P, (2 * u + e + 1) * P)
+                    nc.tensor.matmul_mx(out=y[:, e, :], lhsT=hc[:, cols].bitcast(FP8X4), lhsT_scale=hs[:, cols],
+                                        rhs=gw[h][:].bitcast(FP8X4), rhs_scale=gs[:, half], start=True, stop=True)
+                nc.vector.tensor_tensor(nd[:, pair, half], y[:], n2_t[u][:, :, half], ALU.subtract)
+                nc.scalar.activation(sg[:, pair, half], nd[:, pair, half], ACT.Sigmoid)
 
         wq = keep.tile([P, N, PACK], BF16, name="wq", align_bytes=64)
         wc = keep.tile([P, N], U32, name="wc", align_bytes=64)
@@ -86,6 +91,10 @@ def tile_picked_ylandk_loo_p_kernel(tc, x_words, x_scales, hT, n2, bw, unit, w1,
         nc.vector.tensor_copy(wq[:].rearrange("p (c i) t -> p c t i", i=4), w_raw[:].rearrange("p t (c i) -> p c t i", i=4))
         nc.vector.quantize_mx(out=wc[:].bitcast(FP8X4), scales=ws[:], in_=wq[:].rearrange("p n t -> p (n t)"))
 
+        scaled = keep.tile([P, PACK], F32, name="scaled")
+        runit = keep.tile([P, PACK], F32, name="runit")
+        nc.vector.tensor_scalar(scaled[:], unit_t[:], float(S), None, ALU.mult)
+        nc.vector.reciprocal(runit[:], scaled[:])
         lg = keep.tile([P, PACK, S], F32, name="lg", align_bytes=64)
         ndis = keep.tile([P, PACK, S], F32, name="ndis", align_bytes=64)
         zz = [keep.tile([P, 2 * S], F32, name=f"zz{t}", align_bytes=64) for t in range(PACK)]
@@ -105,47 +114,89 @@ def tile_picked_ylandk_loo_p_kernel(tc, x_words, x_scales, hT, n2, bw, unit, w1,
         ks = [keep.tile([P, S], F32, name=f"ks{t}", align_bytes=64) for t in range(PACK)]
         loo = [keep.tile([P, S], F32, name=f"loo{t}", align_bytes=64) for t in range(PACK)]
         hid = keep.tile([P, PACK, S], BF16, name="hid", align_bytes=64)
-        for pair in range(2):
-            tot = keep.tile([P, 2], F32, name=f"tot{pair}")
-            den = keep.tile([P, 2], F32, name=f"den{pair}")
-            inv = keep.tile([P, 2], F32, name=f"inv{pair}")
-            fac = keep.tile([P, 2], F32, name=f"fac{pair}")
-            t0, t1 = 2 * pair, 2 * pair + 1
-            for u, t in enumerate((t0, t1)):
-                nc.scalar.activation(ker[t][:], zz[t][:, :S], ACT.Sigmoid, accum_out=tot[:, u : u + 1])
-                if t in SCALAR_GATHERS:
-                    nc.scalar.activation(ks[t][:], zz[t][:].indirect(sib_t[:]), ACT.Sigmoid)
-                else:
-                    nc.scalar.activation(ks[t][:], zs[t][:], ACT.Sigmoid)
-            nc.vector.tensor_tensor(loo[t0][:], ker[t0][:], ks[t0][:], ALU.subtract)
-            nc.vector.tensor_scalar(den[:], tot[:], 0.2 * S, None, ALU.add)
-            nc.vector.reciprocal(inv[:], den[:])
-            nc.vector.scalar_tensor_tensor(fac[:], inv[:], float(S), unit_t[:, t0 : t1 + 1], ALU.mult, ALU.mult)
-            nc.vector.tensor_tensor(loo[t1][:], ker[t1][:], ks[t1][:], ALU.subtract)
-            nc.vector.scalar_tensor_tensor(hid[:, t0, :], loo[t0][:], fac[:, 0:1], ker[t0][:], ALU.mult, ALU.mult)
-            halves = (slice(0, S),) if pair == 0 else (slice(0, S // 2), slice(S // 2, S))
-            for cols in halves:
-                nc.vector.scalar_tensor_tensor(hid[:, t1, cols], loo[t1][:, cols], fac[:, 1:2], ker[t1][:, cols], ALU.mult, ALU.mult)
+        groups = ((0, 1), (1, 2), (2, 4))
+        group_of = (0, 1, 2, 2)
+        tot = [keep.tile([P, b - a], F32, name=f"tot{a}") for a, b in groups]
+        den = [keep.tile([P, b - a], F32, name=f"den{a}") for a, b in groups]
+        fac = [keep.tile([P, b - a], F32, name=f"fac{a}") for a, b in groups]
+        last = PACK - 1
+        lo, hi, whole = slice(0, HALF), slice(HALF, S), slice(0, S)
+
+        def column(tiles, t):
+            g = group_of[t]
+            return tiles[g][:, t - groups[g][0] : t - groups[g][0] + 1]
+
+        def kernel_values(t):
+            nc.scalar.activation(ker[t][:], zz[t][:, :S], ACT.Sigmoid, accum_out=column(tot, t))
+
+        def sibling_values(t):
+            nc.scalar.activation(ks[t][:], zs[t][:], ACT.Sigmoid)
+
+        kernel_values(0)
+        sibling_values(0)
+        kernel_values(1)
+        sibling_values(1)
+        kernel_values(2)
+        kernel_values(3)
+        sibling_values(2)
+        for h, cols in enumerate((lo, hi)):
+            nc.scalar.activation(ks[last][:, cols], zz[last][:].indirect(sib_t[:, h * HALF // 16 : (h + 1) * HALF // 16]), ACT.Sigmoid)
+
+        def shift(g):
+            nc.vector.scalar_tensor_tensor(den[g][:], tot[g][:], 0.2 * S, runit[:, groups[g][0] : groups[g][1]], ALU.add, ALU.mult)
+
+        def invert(g):
+            nc.vector.reciprocal(fac[g][:], den[g][:])
+
+        def differ(t, cols):
+            nc.vector.tensor_tensor(loo[t][:, cols], ker[t][:, cols], ks[t][:, cols], ALU.subtract)
+
+        def hidden(t, cols):
+            nc.vector.scalar_tensor_tensor(hid[:, t, cols], loo[t][:, cols], column(fac, t), ker[t][:, cols], ALU.mult, ALU.mult)
+
+        shift(0)
+        invert(0)
+        differ(0, whole)
+        shift(1)
+        hidden(0, whole)
+        invert(1)
+        differ(1, whole)
+        hidden(1, whole)
+        shift(2)
+        invert(2)
+        differ(2, whole)
+        differ(3, lo)
+        hidden(2, lo)
+        hidden(3, lo)
+        differ(3, hi)
+        hidden(2, hi)
+        hidden(3, hi)
 
         res = keep.tile([P, S], F32, name="res", align_bytes=64)
-        woven = [keep.tile([P, CHUNK, PACK], BF16, name=f"woven{c}", align_bytes=64) for c in range(S // CHUNK)]
-        for c in range(S // CHUNK):
-            cols = slice(c * CHUNK, (c + 1) * CHUNK)
-            wdst = woven[c][:].rearrange("p (c i) t -> p c t i", i=4)
-            wsrc = hid[:, :, cols].rearrange("p t (c i) -> p c t i", i=4)
-            if c % 2 == 0:
-                nc.scalar.copy(wdst, wsrc)
-            else:
-                nc.vector.tensor_copy(wdst, wsrc)
-        for c in range(S // CHUNK):
-            cols = slice(c * CHUNK, (c + 1) * CHUNK)
-            qc = keep.tile([P, CHUNK], U32, name=f"qc{c}", align_bytes=64)
-            qs = keep.tile([P, CHUNK], U8, name=f"qs{c}", align_bytes=64)
-            acc = psum.tile([P, CHUNK], F32, name=f"acc{c}")
-            nc.vector.quantize_mx(out=qc[:].bitcast(FP8X4), scales=qs[:], in_=woven[c][:].rearrange("p n t -> p (n t)"))
+        woven = [keep.tile([P, HALF, PACK], BF16, name=f"woven{h}", align_bytes=64) for h in range(2)]
+        qc = [keep.tile([P, HALF], U32, name=f"qc{h}", align_bytes=64) for h in range(2)]
+        qs = [keep.tile([P, HALF], U8, name=f"qs{h}", align_bytes=64) for h in range(2)]
+
+        def weave(engine_copy, h, a, b):
+            engine_copy(woven[h][:, a:b, :].rearrange("p (c i) t -> p c t i", i=4),
+                        hid[:, :, h * HALF + a : h * HALF + b].rearrange("p t (c i) -> p c t i", i=4))
+
+        def quantise(h):
+            nc.vector.quantize_mx(out=qc[h][:].bitcast(FP8X4), scales=qs[h][:], in_=woven[h][:].rearrange("p n t -> p (n t)"))
+
+        def finish(h, a, b, engine_copy, queue):
+            acc = psum.tile([P, b - a], F32, name=f"acc{h}_{a}")
             nc.tensor.matmul_mx(out=acc[:], lhsT=wc[:].bitcast(FP8X4), lhsT_scale=ws[:],
-                                rhs=qc[:].bitcast(FP8X4), rhs_scale=qs[:], start=True, stop=True)
-            nc.scalar.copy(res[:, cols], acc[:])
-            if c % 2 == 1:
-                both = slice((c - 1) * CHUNK, (c + 1) * CHUNK)
-                nc.sync.dma_start(out[:, both], res[:, both])
+                                rhs=qc[h][:, a:b].bitcast(FP8X4), rhs_scale=qs[h][:, a:b], start=True, stop=True)
+            cols = slice(h * HALF + a, h * HALF + b)
+            engine_copy(res[:, cols], acc[:])
+            queue.dma_start(out[:, cols], res[:, cols])
+
+        weave(nc.scalar.copy, 0, 0, HALF)
+        weave(nc.scalar.copy, 1, 0, CHUNK)
+        quantise(0)
+        weave(nc.vector.tensor_copy, 1, CHUNK, HALF)
+        finish(0, 0, HALF, nc.scalar.copy, nc.sync)
+        quantise(1)
+        finish(1, 0, CHUNK, nc.vector.tensor_copy, nc.sync)
+        finish(1, CHUNK, HALF, nc.scalar.copy, nc.scalar)

@@ -36,7 +36,7 @@ def tile_picked_ylandk_loo_p_kernel(tc, x_words, x_scales, hT, n2, bw, unit, w1,
         h_raw = keep.tile([P, PACK, H], F32, name="h_raw", align_bytes=64)
         w_raw = keep.tile([P, PACK, N], F32, name="w_raw", align_bytes=64)
         unit_t = keep.tile([P, PACK], F32, name="unit_t")
-        n2_t = [keep.tile([P, 2, S], F32, name=f"n2_{u}", align_bytes=64) for u in range(2)]
+        n2_t = [keep.tile([P, 2, S], F32, name=f"n2_{u}", tag=f"pair{u}", align_bytes=64) for u in range(2)]
         bw_t = [keep.tile([P, S], F32, name=f"bw_{t}", align_bytes=64) for t in range(PACK)]
 
         nc.vector.memset(xs[:].bitcast(I32), 0)
@@ -60,8 +60,8 @@ def tile_picked_ylandk_loo_p_kernel(tc, x_words, x_scales, hT, n2, bw, unit, w1,
         nc.vector.tensor_copy(gs[:], xs[:].indirect(offs_t[:]))
 
         hq = keep.tile([P, PACK, P, PACK], BF16, name="hq", align_bytes=64)
-        src = h_raw[:].rearrange("p j (m t) -> p m j t", t=PACK)
-        dst = hq[:].rearrange("p t m j -> p m j t")
+        src = h_raw[:].rearrange("p j (m t) -> p m t j", t=PACK)
+        dst = hq[:].rearrange("p t m j -> p m t j")
         cut = 80
         nc.scalar.copy(dst[:, cut:, :, :], src[:, cut:, :, :])
         nc.vector.tensor_copy(dst[:, :cut, :, :], src[:, :cut, :, :])
@@ -82,8 +82,10 @@ def tile_picked_ylandk_loo_p_kernel(tc, x_words, x_scales, hT, n2, bw, unit, w1,
                     cols = slice((2 * u + e) * P, (2 * u + e + 1) * P)
                     nc.tensor.matmul_mx(out=y[:, e, :], lhsT=hc[:, cols].bitcast(FP8X4), lhsT_scale=hs[:, cols],
                                         rhs=gw[h][:].bitcast(FP8X4), rhs_scale=gs[:, half], start=True, stop=True)
-                nc.vector.tensor_tensor(nd[:, pair, half], y[:], n2_t[u][:, :, half], ALU.subtract)
-                nc.scalar.activation(sg[:, pair, half], nd[:, pair, half], ACT.Sigmoid)
+                for rows in ((slice(0, 1), slice(1, 2)) if u + h == 2 else (slice(0, 2),)):
+                    tiles = slice(2 * u + rows.start, 2 * u + rows.stop)
+                    nc.vector.tensor_tensor(nd[:, tiles, half], y[:, rows, :], n2_t[u][:, rows, half], ALU.subtract)
+                    nc.scalar.activation(sg[:, tiles, half], nd[:, tiles, half], ACT.Sigmoid)
 
         wq = keep.tile([P, N, PACK], BF16, name="wq", align_bytes=64)
         wc = keep.tile([P, N], U32, name="wc", align_bytes=64)
@@ -95,20 +97,40 @@ def tile_picked_ylandk_loo_p_kernel(tc, x_words, x_scales, hT, n2, bw, unit, w1,
         runit = keep.tile([P, PACK], F32, name="runit")
         nc.vector.tensor_scalar(scaled[:], unit_t[:], float(S), None, ALU.mult)
         nc.vector.reciprocal(runit[:], scaled[:])
-        lg = keep.tile([P, PACK, S], F32, name="lg", align_bytes=64)
+        lg = [keep.tile([P, 2, S], F32, name=f"lg{u}", tag=f"pair{1 - u}", align_bytes=64) for u in range(2)]
         ndis = keep.tile([P, PACK, S], F32, name="ndis", align_bytes=64)
         zz = [keep.tile([P, 2 * S], F32, name=f"zz{t}", align_bytes=64) for t in range(PACK)]
-        zs = [keep.tile([P, S], F32, name=f"zs{t}", align_bytes=64) for t in range(PACK)]
-        for c in range(S // CHUNK):
-            cols = slice(c * CHUNK, (c + 1) * CHUNK)
-            nc.scalar.activation(lg[:, :, cols], sg[:, :, cols], ACT.Ln, bias=TINY)
-            nc.vector.scalar_tensor_tensor(ndis[:, :, cols], lg[:, :, cols], -TINY, nd[:, :, cols], ALU.min, ALU.min)
-        for t in range(PACK):
+        zs01 = keep.tile([P, 2, S], F32, name="zs01", align_bytes=64)
+        zs = [zs01[:, 0, :], zs01[:, 1, :], sg[:, 3, :]]
+
+        def log_sigmoid(t):
+            nc.scalar.activation(lg[t // 2][:, t % 2, :], sg[:, t, :], ACT.Ln, bias=TINY)
+
+        def distance(t):
+            nc.vector.scalar_tensor_tensor(ndis[:, t, :], lg[t // 2][:, t % 2, :], -TINY, nd[:, t, :], ALU.min, ALU.min)
+
+        def logs(t):
             nc.scalar.activation(sg[:, t, :], bw_t[t][:], ACT.Ln)
             nc.scalar.activation(zz[t][:, S:], ndis[:, t, :], ACT.Ln, scale=-1.0)
+
+        def logit(t):
             nc.vector.tensor_tensor(zz[t][:, :S], sg[:, t, :], zz[t][:, S:], ALU.subtract)
-            if t not in SCALAR_GATHERS:
-                nc.vector.tensor_copy(zs[t][:], zz[t][:].indirect(sib_t[:]))
+
+        def fetch(t):
+            nc.vector.tensor_copy(zs[t], zz[t][:].indirect(sib_t[:]))
+
+        log_sigmoid(0)
+        distance(0)
+        log_sigmoid(1)
+        distance(1)
+        for t in range(PACK):
+            logs(t)
+            logit(t)
+            if t + 2 < PACK:
+                log_sigmoid(t + 2)
+                distance(t + 2)
+                fetch(t)
+        fetch(2)
 
         ker = [keep.tile([P, S], F32, name=f"ker{t}", align_bytes=64) for t in range(PACK)]
         ks = [keep.tile([P, S], F32, name=f"ks{t}", align_bytes=64) for t in range(PACK)]
@@ -130,7 +152,7 @@ def tile_picked_ylandk_loo_p_kernel(tc, x_words, x_scales, hT, n2, bw, unit, w1,
             nc.scalar.activation(ker[t][:], zz[t][:, :S], ACT.Sigmoid, accum_out=column(tot, t))
 
         def sibling_values(t):
-            nc.scalar.activation(ks[t][:], zs[t][:], ACT.Sigmoid)
+            nc.scalar.activation(ks[t][:], zs[t], ACT.Sigmoid)
 
         kernel_values(0)
         sibling_values(0)
@@ -163,8 +185,8 @@ def tile_picked_ylandk_loo_p_kernel(tc, x_words, x_scales, hT, n2, bw, unit, w1,
         differ(1, whole)
         hidden(1, whole)
         shift(2)
-        invert(2)
         differ(2, whole)
+        invert(2)
         differ(3, lo)
         hidden(2, lo)
         hidden(3, lo)
@@ -173,30 +195,26 @@ def tile_picked_ylandk_loo_p_kernel(tc, x_words, x_scales, hT, n2, bw, unit, w1,
         hidden(3, hi)
 
         res = keep.tile([P, S], F32, name="res", align_bytes=64)
-        woven = [keep.tile([P, HALF, PACK], BF16, name=f"woven{h}", align_bytes=64) for h in range(2)]
-        qc = [keep.tile([P, HALF], U32, name=f"qc{h}", align_bytes=64) for h in range(2)]
-        qs = [keep.tile([P, HALF], U8, name=f"qs{h}", align_bytes=64) for h in range(2)]
+        woven = keep.tile([P, S, PACK], BF16, name="woven", align_bytes=64)
 
-        def weave(engine_copy, h, a, b):
-            engine_copy(woven[h][:, a:b, :].rearrange("p (c i) t -> p c t i", i=4),
-                        hid[:, :, h * HALF + a : h * HALF + b].rearrange("p t (c i) -> p c t i", i=4))
+        def weave(engine_copy, place, a, b):
+            engine_copy(woven[:, place : place + b - a, :].rearrange("p (c i) t -> p c t i", i=4),
+                        hid[:, :, a:b].rearrange("p t (c i) -> p c t i", i=4))
 
-        def quantise(h):
-            nc.vector.quantize_mx(out=qc[h][:].bitcast(FP8X4), scales=qs[h][:], in_=woven[h][:].rearrange("p n t -> p (n t)"))
-
-        def finish(h, a, b, engine_copy, queue):
-            acc = psum.tile([P, b - a], F32, name=f"acc{h}_{a}")
+        def finish(place, a, b, engine_copy):
+            qc = keep.tile([P, b - a], U32, name=f"qc{a}", align_bytes=64)
+            qs = keep.tile([P, b - a], U8, name=f"qs{a}", align_bytes=64)
+            acc = psum.tile([P, b - a], F32, name=f"acc{a}")
+            nc.vector.quantize_mx(out=qc[:].bitcast(FP8X4), scales=qs[:], in_=woven[:, place : place + b - a, :].rearrange("p n t -> p (n t)"))
             nc.tensor.matmul_mx(out=acc[:], lhsT=wc[:].bitcast(FP8X4), lhsT_scale=ws[:],
-                                rhs=qc[h][:, a:b].bitcast(FP8X4), rhs_scale=qs[h][:, a:b], start=True, stop=True)
-            cols = slice(h * HALF + a, h * HALF + b)
-            engine_copy(res[:, cols], acc[:])
-            queue.dma_start(out[:, cols], res[:, cols])
+                                rhs=qc[:].bitcast(FP8X4), rhs_scale=qs[:], start=True, stop=True)
+            engine_copy(res[:, a:b], acc[:])
 
         weave(nc.scalar.copy, 0, 0, HALF)
-        weave(nc.scalar.copy, 1, 0, CHUNK)
-        quantise(0)
-        weave(nc.vector.tensor_copy, 1, CHUNK, HALF)
-        finish(0, 0, HALF, nc.scalar.copy, nc.sync)
-        quantise(1)
-        finish(1, 0, CHUNK, nc.vector.tensor_copy, nc.sync)
-        finish(1, CHUNK, HALF, nc.scalar.copy, nc.scalar)
+        weave(nc.scalar.copy, HALF, HALF, HALF + CHUNK)
+        weave(nc.vector.tensor_copy, HALF + CHUNK, HALF + CHUNK, S)
+        finish(0, 0, HALF, nc.scalar.copy)
+        nc.sync.dma_start(out[:, lo], res[:, lo])
+        finish(HALF + CHUNK, HALF + CHUNK, S, nc.scalar.copy)
+        finish(HALF, HALF, HALF + CHUNK, nc.vector.tensor_copy)
+        nc.sync.dma_start(out[:, hi], res[:, hi])

from contextlib import ExitStack

import concourse.mybir as mybir

K, T, S, N, H = 512, 2048, 512, 128, 512
FLOPS = 2 * K * H * S + 2 * H * N * S

F32 = mybir.dt.float32
BF16 = mybir.dt.bfloat16
I32 = mybir.dt.int32
U32 = mybir.dt.uint32
U16 = mybir.dt.uint16
U8 = mybir.dt.uint8
FP8X4 = mybir.dt.float8_e4m3fn_x4
ALU = mybir.AluOpType
ACT = mybir.ActivationFunctionType

P = 128
PACK = 4
TINY = 2.0 ** -60
CHUNK = 128
HALF = S // 2
SCALAR_GATHERS = (3,)


def tile_picked_ylandk_loo_p_kernel(tc, x_words, x_scales, hT, n2, bw, unit, w1, offs, sib, out):
    nc = tc.nc
    with ExitStack() as ctx:
        keep = ctx.enter_context(tc.tile_pool(name="keep", bufs=1))
        psum = ctx.enter_context(tc.psum_pool(name="psum", bufs=1))

        offs_t = keep.tile([P, S // 16], U16, name="offs_t")
        sib_t = keep.tile([P, S // 16], U16, name="sib_t")
        xw = keep.tile([P, T], U32, name="xw", align_bytes=64)
        xs = keep.tile([P, T], U8, name="xs", align_bytes=64)
        h_raw = keep.tile([P, PACK, H], F32, name="h_raw", align_bytes=64)
        w_raw = keep.tile([P, PACK, N], F32, name="w_raw", align_bytes=64)
        unit_t = keep.tile([P, PACK], F32, name="unit_t")
        n2_t = [keep.tile([P, 2, S], F32, name=f"n2_{u}", tag=f"pair{u}", align_bytes=64) for u in range(2)]
        bw_t = [keep.tile([P, S], F32, name=f"bw_{t}", align_bytes=64) for t in range(PACK)]

        nc.vector.memset(xs[:].bitcast(I32), 0)
        nc.sync.dma_start(offs_t[:], offs)
        nc.sync.dma_start(h_raw[:], hT.rearrange("(p j) c -> p j c", j=PACK))
        for q in range(4):
            nc.sync.dma_start(xs[32 * q : 32 * q + 4, :].bitcast(I32), x_scales[0, 4 * q : 4 * q + 4, :].bitcast(I32))
        nc.sync.dma_start(xw[:].bitcast(I32), x_words[0].rearrange("p n r -> p (n r)").bitcast(I32))
        n2_v = n2.rearrange("(p t) j -> p t j", t=PACK)
        bw_v = bw.rearrange("(p t) j -> p t j", t=PACK)
        for u in range(2):
            nc.sync.dma_start(n2_t[u][:], n2_v[:, 2 * u : 2 * u + 2, :])
        nc.sync.dma_start(w_raw[:], w1.rearrange("(p t) n -> p t n", t=PACK))
        nc.sync.dma_start(unit_t[:], unit.rearrange("(p t) o -> p (t o)", t=PACK))
        for t in range(PACK):
            nc.sync.dma_start(bw_t[t][:], bw_v[:, t, :])
        nc.sync.dma_start(sib_t[:], sib)

        gs = keep.tile([P, S], U8, name="gs", align_bytes=64)
        gw = [keep.tile([P, HALF], U32, name=f"gw{h}", align_bytes=64) for h in range(2)]
        nc.vector.tensor_copy(gs[:], xs[:].indirect(offs_t[:]))

        hq = keep.tile([P, PACK, P, PACK], BF16, name="hq", align_bytes=64)
        src = h_raw[:].rearrange("p j (m t) -> p m t j", t=PACK)
        dst = hq[:].rearrange("p t m j -> p m t j")
        cut = 80
        nc.scalar.copy(dst[:, cut:, :, :], src[:, cut:, :, :])
        nc.vector.tensor_copy(dst[:, :cut, :, :], src[:, :cut, :, :])
        hc = keep.tile([P, H], U32, name="hc", align_bytes=64)
        hs = keep.tile([P, H], U8, name="hs", align_bytes=64)
        nc.vector.quantize_mx(out=hc[:].bitcast(FP8X4), scales=hs[:], in_=hq[:].rearrange("p t m j -> p (t m j)"))
        for h in range(2):
            nc.vector.tensor_copy(gw[h][:], xw[:].indirect(offs_t[:, h * HALF // 16 : (h + 1) * HALF // 16]))

        nd = keep.tile([P, PACK, S], F32, name="nd", align_bytes=64)
        sg = keep.tile([P, PACK, S], F32, name="sg", align_bytes=64)
        for u in range(2):
            pair = slice(2 * u, 2 * u + 2)
            for h in range(2):
                half = slice(h * HALF, (h + 1) * HALF)
                y = psum.tile([P, 2, HALF], F32, name=f"y{u}{h}")
                for e in range(2):
                    cols = slice((2 * u + e) * P, (2 * u + e + 1) * P)
                    nc.tensor.matmul_mx(out=y[:, e, :], lhsT=hc[:, cols].bitcast(FP8X4), lhsT_scale=hs[:, cols],
                                        rhs=gw[h][:].bitcast(FP8X4), rhs_scale=gs[:, half], start=True, stop=True)
                for rows in ((slice(0, 1), slice(1, 2)) if u + h == 2 else (slice(0, 2),)):
                    tiles = slice(2 * u + rows.start, 2 * u + rows.stop)
                    nc.vector.tensor_tensor(nd[:, tiles, half], y[:, rows, :], n2_t[u][:, rows, half], ALU.subtract)
                    nc.scalar.activation(sg[:, tiles, half], nd[:, tiles, half], ACT.Sigmoid)

        wq = keep.tile([P, N, PACK], BF16, name="wq", align_bytes=64)
        wc = keep.tile([P, N], U32, name="wc", align_bytes=64)
        ws = keep.tile([P, N], U8, name="ws", align_bytes=64)
        nc.vector.tensor_copy(wq[:].rearrange("p (c i) t -> p c t i", i=4), w_raw[:].rearrange("p t (c i) -> p c t i", i=4))
        nc.vector.quantize_mx(out=wc[:].bitcast(FP8X4), scales=ws[:], in_=wq[:].rearrange("p n t -> p (n t)"))

        scaled = keep.tile([P, PACK], F32, name="scaled")
        runit = keep.tile([P, PACK], F32, name="runit")
        nc.vector.tensor_scalar(scaled[:], unit_t[:], float(S), None, ALU.mult)
        nc.vector.reciprocal(runit[:], scaled[:])
        lg = [keep.tile([P, 2, S], F32, name=f"lg{u}", tag=f"pair{1 - u}", align_bytes=64) for u in range(2)]
        ndis = keep.tile([P, PACK, S], F32, name="ndis", align_bytes=64)
        zz = [keep.tile([P, 2 * S], F32, name=f"zz{t}", align_bytes=64) for t in range(PACK)]
        zs01 = keep.tile([P, 2, S], F32, name="zs01", align_bytes=64)
        zs = [zs01[:, 0, :], zs01[:, 1, :], sg[:, 3, :]]

        def log_sigmoid(t):
            nc.scalar.activation(lg[t // 2][:, t % 2, :], sg[:, t, :], ACT.Ln, bias=TINY)

        def distance(t):
            nc.vector.scalar_tensor_tensor(ndis[:, t, :], lg[t // 2][:, t % 2, :], -TINY, nd[:, t, :], ALU.min, ALU.min)

        def logs(t):
            nc.scalar.activation(sg[:, t, :], bw_t[t][:], ACT.Ln)
            nc.scalar.activation(zz[t][:, S:], ndis[:, t, :], ACT.Ln, scale=-1.0)

        def logit(t):
            nc.vector.tensor_tensor(zz[t][:, :S], sg[:, t, :], zz[t][:, S:], ALU.subtract)

        def fetch(t):
            nc.vector.tensor_copy(zs[t], zz[t][:].indirect(sib_t[:]))

        log_sigmoid(0)
        distance(0)
        log_sigmoid(1)
        distance(1)
        for t in range(PACK):
            logs(t)
            logit(t)
            if t + 2 < PACK:
                log_sigmoid(t + 2)
                distance(t + 2)
                fetch(t)
        fetch(2)

        ker = [keep.tile([P, S], F32, name=f"ker{t}", align_bytes=64) for t in range(PACK)]
        ks = [keep.tile([P, S], F32, name=f"ks{t}", align_bytes=64) for t in range(PACK)]
        loo = [keep.tile([P, S], F32, name=f"loo{t}", align_bytes=64) for t in range(PACK)]
        hid = keep.tile([P, PACK, S], BF16, name="hid", align_bytes=64)
        groups = ((0, 1), (1, 2), (2, 4))
        group_of = (0, 1, 2, 2)
        tot = [keep.tile([P, b - a], F32, name=f"tot{a}") for a, b in groups]
        den = [keep.tile([P, b - a], F32, name=f"den{a}") for a, b in groups]
        fac = [keep.tile([P, b - a], F32, name=f"fac{a}") for a, b in groups]
        last = PACK - 1
        lo, hi, whole = slice(0, HALF), slice(HALF, S), slice(0, S)

        def column(tiles, t):
            g = group_of[t]
            return tiles[g][:, t - groups[g][0] : t - groups[g][0] + 1]

        def kernel_values(t):
            nc.scalar.activation(ker[t][:], zz[t][:, :S], ACT.Sigmoid, accum_out=column(tot, t))

        def sibling_values(t):
            nc.scalar.activation(ks[t][:], zs[t], ACT.Sigmoid)

        kernel_values(0)
        sibling_values(0)
        kernel_values(1)
        sibling_values(1)
        kernel_values(2)
        kernel_values(3)
        sibling_values(2)
        for h, cols in enumerate((lo, hi)):
            nc.scalar.activation(ks[last][:, cols], zz[last][:].indirect(sib_t[:, h * HALF // 16 : (h + 1) * HALF // 16]), ACT.Sigmoid)

        def shift(g):
            nc.vector.scalar_tensor_tensor(den[g][:], tot[g][:], 0.2 * S, runit[:, groups[g][0] : groups[g][1]], ALU.add, ALU.mult)

        def invert(g):
            nc.vector.reciprocal(fac[g][:], den[g][:])

        def differ(t, cols):
            nc.vector.tensor_tensor(loo[t][:, cols], ker[t][:, cols], ks[t][:, cols], ALU.subtract)

        def hidden(t, cols):
            nc.vector.scalar_tensor_tensor(hid[:, t, cols], loo[t][:, cols], column(fac, t), ker[t][:, cols], ALU.mult, ALU.mult)

        shift(0)
        invert(0)
        differ(0, whole)
        shift(1)
        hidden(0, whole)
        invert(1)
        differ(1, whole)
        hidden(1, whole)
        shift(2)
        differ(2, whole)
        invert(2)
        differ(3, lo)
        hidden(2, lo)
        hidden(3, lo)
        differ(3, hi)
        hidden(2, hi)
        hidden(3, hi)

        res = keep.tile([P, S], F32, name="res", align_bytes=64)
        woven = keep.tile([P, S, PACK], BF16, name="woven", align_bytes=64)

        def weave(engine_copy, place, a, b):
            engine_copy(woven[:, place : place + b - a, :].rearrange("p (c i) t -> p c t i", i=4),
                        hid[:, :, a:b].rearrange("p t (c i) -> p c t i", i=4))

        def finish(place, a, b, engine_copy):
            qc = keep.tile([P, b - a], U32, name=f"qc{a}", align_bytes=64)
            qs = keep.tile([P, b - a], U8, name=f"qs{a}", align_bytes=64)
            acc = psum.tile([P, b - a], F32, name=f"acc{a}")
            nc.vector.quantize_mx(out=qc[:].bitcast(FP8X4), scales=qs[:], in_=woven[:, place : place + b - a, :].rearrange("p n t -> p (n t)"))
            nc.tensor.matmul_mx(out=acc[:], lhsT=wc[:].bitcast(FP8X4), lhsT_scale=ws[:],
                                rhs=qc[:].bitcast(FP8X4), rhs_scale=qs[:], start=True, stop=True)
            engine_copy(res[:, a:b], acc[:])

        weave(nc.scalar.copy, 0, 0, HALF)
        weave(nc.scalar.copy, HALF, HALF, HALF + CHUNK)
        weave(nc.vector.tensor_copy, HALF + CHUNK, HALF + CHUNK, S)
        finish(0, 0, HALF, nc.scalar.copy)
        nc.sync.dma_start(out[:, lo], res[:, lo])
        finish(HALF + CHUNK, HALF + CHUNK, S, nc.scalar.copy)
        finish(HALF, HALF, HALF + CHUNK, nc.vector.tensor_copy)
        nc.sync.dma_start(out[:, hi], res[:, hi])
